import numpy as np, ml_dtypes
CORES = [5,29,101,125,133,157,229,253]
N = 8
C = 128
SIGN = [[1,1,1,1,1,1,1,1],[1,-1,1,-1,1,-1,1,-1],[1,1,-1,-1,1,1,-1,-1],[1,-1,-1,1,1,-1,-1,1],[1,1,1,1,-1,-1,-1,-1],[1,-1,1,-1,-1,1,-1,1],[1,1,-1,-1,-1,-1,1,1],[1,-1,-1,1,-1,1,1,-1]]
def setup_inputs(rng):
    return {"x": rng.standard_normal((N, 128, C), dtype=np.float32).astype(ml_dtypes.bfloat16), "w": (rng.standard_normal((N, 128, 128), dtype=np.float32) / 11).astype(ml_dtypes.bfloat16)}
def setup_inputs_big(rng):
    d = setup_inputs(rng)
    for k in ("x", "w"): d[k] = (d[k].astype(np.float32) * 1024.0).astype(d[k].dtype)
    return d
def setup_inputs_small(rng):
    d = setup_inputs(rng)
    for k in ("x", "w"): d[k] = (d[k].astype(np.float32) * (1 / 1024.0)).astype(d[k].dtype)
    return d
def setup_inputs_apart(rng):
    d = setup_inputs(rng)
    f = (10.0 ** rng.permutation(np.linspace(-1.5, 1.5, N))).astype(np.float32).reshape(N, 1, 1)
    for k in ("x", "w"): d[k] = (d[k].astype(np.float32) * f).astype(d[k].dtype)
    return d
def reference(x, w):
    X = x.astype(np.float64)
    y = np.stack([w[r].astype(np.float64).T @ sum(SIGN[r][j] * X[j] for j in range(N)) for r in range(N)])
    return {"y": y.astype(ml_dtypes.bfloat16)}

@@ -1,0 +1,151 @@
+from concourse.bass import DstId, RemoteDMATransfer
+from concourse.mybir import AluOpType
+
+N = 8
+C = 128
+
+SCRATCH = {
+    "xd": ("dram", [128, C], "bfloat16"),
+    "xs": ("sbuf", [128, C], "bfloat16"),
+    "ws": ("sbuf", [128, C], "bfloat16"),
+    "wn": ("sbuf", [128, C], "bfloat16"),
+    "m1": ("sbuf", [128, C], "bfloat16"),
+    "land": ("sbuf", [128, N * C], "bfloat16"),
+    "ps": ("psum", [128, C], "float32"),
+    "ys": ("sbuf", [128, C], "bfloat16"),
+}
+SEMAPHORES = ["xdl", "xsl", "wl", "ms", "ng", "got", "sent", "mm", "cp", "st"] + ["a%d" % j for j in range(N)]
+
+HOP1_ENGINES = 2
+
+
+def _bits(mask):
+    return [e for e in range(mask.bit_length()) if (mask >> e) & 1]
+
+
+def _mask(engines):
+    m = 0
+    for e in engines:
+        m |= 1 << e
+    return m
+
+
+def _same_chip(topo, a, b):
+    return topo.host(a) == topo.host(b) and topo.chip(a) == topo.chip(b)
+
+
+def _plan(T, topo, s):
+    cores = list(T.cores)
+    world = range(topo.CORES_PER_HOST * (1 + max(topo.host(c) for c in cores)))
+    plane = [d for d in cores if d != s and topo.may_write(s, d)]
+    cross = [d for d in cores if d != s and not topo.may_write(s, d)]
+    port = [k for k in world if k != s and _same_chip(topo, k, s) and all(topo.may_write(k, d) for d in cross)]
+    near = [k for k in port if topo.die(k) == topo.die(s)]
+    far = [k for k in port if topo.die(k) != topo.die(s)]
+    order = []
+    for i in range(max(len(near), len(far))):
+        order += near[i:i + 1] + far[i:i + 1]
+    turn = sorted([s] + plane).index(s)
+    via = {}
+    for a, d in enumerate(cross):
+        via[d] = order[(a + turn) % len(order)]
+    return plane, cross, order, via
+
+
+def rank_program(g, core, T, topo):
+    cores = list(T.cores)
+    owner = [s for s in cores if _same_chip(topo, s, core)]
+    if not owner:
+        return
+    s = owner[0]
+    plane, cross, order, via = _plan(T, topo, s)
+    sem = T.sem
+    j_own = T.rank_of(s)
+    slot = T.land[:, j_own * C:(j_own + 1) * C]
+
+    if core != s:
+        mine = [d for d in cross if via[d] == core]
+        if not mine:
+            return
+        g.wait_ge(sem.got, HOP1_ENGINES)
+        total = 0
+        for d in mine:
+            rid, pid = topo.addr(d, core)
+            m = topo.mask(core, d)
+            g.remote_dma(slot, T.xd[:, :], sem["a%d" % j_own], sem.sent, pid, rid, m)
+            total += len(_bits(m))
+        g.wait_ge(sem.sent, total)
+        return
+
+    r = j_own
+    sign = T.tables["SIGN"][r]
+    sy, te, ve = g.sync, g.tensor, g.vector
+
+    sy.dma_start(T.xd[:, :], T.x[:, :]).then_inc(sem.xdl, 16)
+    sy.dma_start(T.ws[:, :], T.w[:, :]).then_inc(sem.wl, 16)
+    sy.dma_start(T.xs[:, :], T.x[:, :]).then_inc(sem.xsl, 16)
+
+    need_neg = any(v < 0 for v in sign)
+    if need_neg:
+        ve.memset(T.m1[:, :], -1.0).then_inc(sem.ms, 1)
+        ve.wait_ge(sem.ms, 1)
+        ve.wait_ge(sem.wl, 16)
+        ve.tensor_tensor(T.wn[:, :], T.ws[:, :], T.m1[:, :], AluOpType.mult).then_inc(sem.ng, 1)
+
+    out_mask = topo.mask(s, plane[0])
+    for d in plane:
+        out_mask &= topo.mask(s, d)
+    used = [h for h in order if h in via.values()]
+    for h in used:
+        out_mask &= topo.mask(s, h)
+    eng = _bits(out_mask)
+    g.wait_ge(sem.xdl, 16)
+    sent = 0
+    hop1 = []
+    group = 2 * HOP1_ENGINES
+    for q, h in enumerate(used):
+        base = (q // 2) * group + (q % 2)
+        mine = [eng[(base + 2 * i) % len(eng)] for i in range(HOP1_ENGINES)]
+        rid, pid = topo.addr(h, s)
+        hop1.append(RemoteDMATransfer(dst_ids=[DstId(rid=rid, pnc=pid)], dma_engine_mask=_mask(mine),
+                                      remote_sem=sem.got, src=T.xd[:, :], dst=T.xd[:, :]))
+        sent += len(mine)
+    g.remote_dma_fused(hop1, local_sem=sem.sent)
+
+    ids = []
+    for d in plane:
+        rid, pid = topo.addr(d, s)
+        ids.append(DstId(rid=rid, pnc=pid))
+    g.remote_dma_fused([RemoteDMATransfer(dst_ids=ids, dma_engine_mask=out_mask, remote_sem=sem["a%d" % r],
+                                          srcs=[T.xd[:, :]], dsts=[slot for _ in plane])], local_sem=sem.sent)
+    sent += len(eng)
+
+    def stationary(j):
+        return T.ws[:, :] if sign[j] > 0 else T.wn[:, :]
+
+    arrivals = []
+    for d in plane:
+        arrivals.append((T.rank_of(d), len(eng)))
+    late = []
+    for d in cross:
+        h = _plan(T, topo, d)[3][s]
+        late.append((0 if topo.die(h) == topo.die(s) else 1, T.rank_of(d), len(_bits(topo.mask(h, s)))))
+    for _, j, n in sorted(late):
+        arrivals.append((j, n))
+
+    te.wait_ge(sem.wl, 16)
+    te.wait_ge(sem.xsl, 16)
+    if need_neg:
+        te.wait_ge(sem.ng, 1)
+    te.matmul(T.ps[:, :], stationary(r), T.xs[:, :], start=True, stop=False).then_inc(sem.mm, 1)
+    for i, (j, n) in enumerate(arrivals):
+        te.wait_ge(sem["a%d" % j], n)
+        te.matmul(T.ps[:, :], stationary(j), T.land[:, j * C:(j + 1) * C], start=False,
+                  stop=(i == len(arrivals) - 1)).then_inc(sem.mm, 1)
+
+    ve.wait_ge(sem.mm, 1 + len(arrivals))
+    ve.tensor_copy(T.ys[:, :], T.ps[:, :]).then_inc(sem.cp, 1)
+    sy.wait_ge(sem.cp, 1)
+    sy.dma_start(T.y[:, :], T.ys[:, :]).then_inc(sem.st, 16)
+    sy.wait_ge(sem.st, 16)
+    g.wait_ge(sem.sent, sent)

@@ -3,20 +3,28 @@ from concourse.mybir import AluOpType
 
 N = 8
 C = 128
+H = 4
+HALF = C // 2
+NDRAM = 1
 
 SCRATCH = {
+    "hd": ("dram", [128, H], "bfloat16"),
+    "bd": ("dram", [128, C - H], "bfloat16"),
     "xd": ("dram", [128, C], "bfloat16"),
+    "pl": ("dram", [NDRAM * 128, C], "bfloat16"),
     "xs": ("sbuf", [128, C], "bfloat16"),
     "ws": ("sbuf", [128, C], "bfloat16"),
     "wn": ("sbuf", [128, C], "bfloat16"),
     "m1": ("sbuf", [128, C], "bfloat16"),
     "land": ("sbuf", [128, N * C], "bfloat16"),
-    "ps": ("psum", [128, C], "float32"),
+    "pa": ("psum", [128, 512], "float32"),
+    "pb": ("psum", [128, 512], "float32"),
     "ys": ("sbuf", [128, C], "bfloat16"),
 }
-SEMAPHORES = ["xdl", "xsl", "wl", "ms", "ng", "got", "sent", "mm", "cp", "st"] + ["a%d" % j for j in range(N)]
+SEMAPHORES = (["hl", "bl", "xdl", "xsl", "wl", "ms", "ng", "gh", "gb", "sent", "ma", "mb", "cp", "st"]
+              + ["a%d" % j for j in range(N)] + ["sp%d" % i for i in range(NDRAM)])
 
-HOP1_ENGINES = 2
+BODY_ENGINES = 2
 
 
 def _bits(mask):
@@ -37,7 +45,9 @@ def _same_chip(topo, a, b):
 def _plan(T, topo, s):
     cores = list(T.cores)
     world = range(topo.CORES_PER_HOST * (1 + max(topo.host(c) for c in cores)))
-    plane = [d for d in cores if d != s and topo.may_write(s, d)]
+    ring = sorted([s] + [d for d in cores if d != s and topo.may_write(s, d)])
+    turn = ring.index(s)
+    plane = [ring[(turn + i) % len(ring)] for i in range(1, len(ring))]
     cross = [d for d in cores if d != s and not topo.may_write(s, d)]
     port = [k for k in world if k != s and _same_chip(topo, k, s) and all(topo.may_write(k, d) for d in cross)]
     near = [k for k in port if topo.die(k) == topo.die(s)]
@@ -45,7 +55,6 @@ def _plan(T, topo, s):
     order = []
     for i in range(max(len(near), len(far))):
         order += near[i:i + 1] + far[i:i + 1]
-    turn = sorted([s] + plane).index(s)
     via = {}
     for a, d in enumerate(cross):
         via[d] = order[(a + turn) % len(order)]
@@ -61,29 +70,39 @@ def rank_program(g, core, T, topo):
     plane, cross, order, via = _plan(T, topo, s)
     sem = T.sem
     j_own = T.rank_of(s)
-    slot = T.land[:, j_own * C:(j_own + 1) * C]
+    lo = j_own * C
+    slot = T.land[:, lo:lo + C]
 
     if core != s:
         mine = [d for d in cross if via[d] == core]
         if not mine:
             return
-        g.wait_ge(sem.got, HOP1_ENGINES)
         total = 0
+        g.wait_ge(sem.gh, 1)
         for d in mine:
             rid, pid = topo.addr(d, core)
             m = topo.mask(core, d)
-            g.remote_dma(slot, T.xd[:, :], sem["a%d" % j_own], sem.sent, pid, rid, m)
+            g.remote_dma(T.land[:, lo:lo + H], T.hd[:, :], sem["a%d" % j_own], sem.sent, pid, rid, m)
+            total += len(_bits(m))
+        g.wait_ge(sem.gb, BODY_ENGINES)
+        for d in mine:
+            rid, pid = topo.addr(d, core)
+            m = topo.mask(core, d)
+            g.remote_dma(T.land[:, lo + H:lo + C], T.bd[:, :], sem["a%d" % j_own], sem.sent, pid, rid, m)
             total += len(_bits(m))
         g.wait_ge(sem.sent, total)
         return
 
     r = j_own
     sign = T.tables["SIGN"][r]
-    sy, te, ve = g.sync, g.tensor, g.vector
+    sy, sc, te, ve = g.sync, g.scalar, g.tensor, g.vector
 
+    sy.dma_start(T.hd[:, :], T.x[:, 0:H]).then_inc(sem.hl, 16)
     sy.dma_start(T.xd[:, :], T.x[:, :]).then_inc(sem.xdl, 16)
-    sy.dma_start(T.ws[:, :], T.w[:, :]).then_inc(sem.wl, 16)
-    sy.dma_start(T.xs[:, :], T.x[:, :]).then_inc(sem.xsl, 16)
+    sy.dma_start(T.bd[:, :], T.x[:, H:C]).then_inc(sem.bl, 16)
+    sc.wait_ge(sem.hl, 16)
+    sc.dma_start(T.ws[:, :], T.w[:, :]).then_inc(sem.wl, 16)
+    sc.dma_start(T.xs[:, :], T.x[:, :]).then_inc(sem.xsl, 16)
 
     need_neg = any(v < 0 for v in sign)
     if need_neg:
@@ -92,60 +111,95 @@ def rank_program(g, core, T, topo):
         ve.wait_ge(sem.wl, 16)
         ve.tensor_tensor(T.wn[:, :], T.ws[:, :], T.m1[:, :], AluOpType.mult).then_inc(sem.ng, 1)
 
+    used = [h for h in order if h in via.values()]
     out_mask = topo.mask(s, plane[0])
     for d in plane:
         out_mask &= topo.mask(s, d)
-    used = [h for h in order if h in via.values()]
+    chip_mask = topo.mask(s, used[0])
     for h in used:
-        out_mask &= topo.mask(s, h)
-    eng = _bits(out_mask)
-    g.wait_ge(sem.xdl, 16)
+        chip_mask &= topo.mask(s, h)
+    eng = _bits(out_mask & chip_mask)
+    inner = _bits(chip_mask & ~out_mask)
     sent = 0
-    hop1 = []
-    group = 2 * HOP1_ENGINES
-    for q, h in enumerate(used):
-        base = (q // 2) * group + (q % 2)
-        mine = [eng[(base + 2 * i) % len(eng)] for i in range(HOP1_ENGINES)]
-        rid, pid = topo.addr(h, s)
-        hop1.append(RemoteDMATransfer(dst_ids=[DstId(rid=rid, pnc=pid)], dma_engine_mask=_mask(mine),
-                                      remote_sem=sem.got, src=T.xd[:, :], dst=T.xd[:, :]))
-        sent += len(mine)
-    g.remote_dma_fused(hop1, local_sem=sem.sent)
 
     ids = []
-    for d in plane:
+    for h in used:
+        rid, pid = topo.addr(h, s)
+        ids.append(DstId(rid=rid, pnc=pid))
+    g.wait_ge(sem.hl, 16)
+    g.remote_dma_fused([RemoteDMATransfer(dst_ids=ids, dma_engine_mask=_mask(eng[:1]), remote_sem=sem.gh,
+                                          srcs=[T.hd[:, :]], dsts=[T.hd[:, :] for _ in used])], local_sem=sem.sent)
+    sent += 1
+
+    ids = []
+    dsts = []
+    for i, d in enumerate(plane):
         rid, pid = topo.addr(d, s)
         ids.append(DstId(rid=rid, pnc=pid))
-    g.remote_dma_fused([RemoteDMATransfer(dst_ids=ids, dma_engine_mask=out_mask, remote_sem=sem["a%d" % r],
-                                          srcs=[T.xd[:, :]], dsts=[slot for _ in plane])], local_sem=sem.sent)
+        dsts.append(T.pl[i * 128:(i + 1) * 128, :] if i < NDRAM else slot)
+    g.wait_ge(sem.xdl, 16)
+    g.remote_dma_fused([RemoteDMATransfer(dst_ids=ids, dma_engine_mask=_mask(eng), remote_sem=sem["a%d" % r],
+                                          srcs=[T.xd[:, :]], dsts=dsts)], local_sem=sem.sent)
     sent += len(eng)
+
+    g.wait_ge(sem.bl, 16)
+    body = []
+    group = 2 * BODY_ENGINES
+    for q, h in enumerate(used):
+        base = (q // 2) * group + (q % 2)
+        mine = [inner[(base + 2 * i) % len(inner)] for i in range(BODY_ENGINES)]
+        rid, pid = topo.addr(h, s)
+        body.append(RemoteDMATransfer(dst_ids=[DstId(rid=rid, pnc=pid)], dma_engine_mask=_mask(mine),
+                                      remote_sem=sem.gb, src=T.bd[:, :], dst=T.bd[:, :]))
+        sent += len(mine)
+    g.remote_dma_fused(body, local_sem=sem.sent)
+
+    before = list(reversed(plane))
+    queues = [sy, sc]
+    arrivals = []
+    spread = []
+    for i, d in enumerate(before):
+        j = T.rank_of(d)
+        if i < NDRAM:
+            q = queues[i % len(queues)]
+            q.wait_ge(sem["a%d" % j], len(eng))
+            q.dma_start(T.land[:, j * C:(j + 1) * C], T.pl[i * 128:(i + 1) * 128, :]).then_inc(sem["sp%d" % i], 16)
+            spread.append((j, sem["sp%d" % i], 16))
+        else:
+            arrivals.append((j, sem["a%d" % j], len(eng)))
+    arrivals += spread
+
+    late = []
+    for d in cross:
+        _, _, order_d, via_d = _plan(T, topo, d)
+        h = via_d[s]
+        late.append((order_d.index(h), T.rank_of(d), 2 * len(_bits(topo.mask(h, s)))))
+    for _, j, n in sorted(late):
+        arrivals.append((j, sem["a%d" % j], n))
 
     def stationary(j):
         return T.ws[:, :] if sign[j] > 0 else T.wn[:, :]
 
-    arrivals = []
-    for d in plane:
-        arrivals.append((T.rank_of(d), len(eng)))
-    late = []
-    for d in cross:
-        h = _plan(T, topo, d)[3][s]
-        late.append((0 if topo.die(h) == topo.die(s) else 1, T.rank_of(d), len(_bits(topo.mask(h, s)))))
-    for _, j, n in sorted(late):
-        arrivals.append((j, n))
+    def product(j, xap_base, buf, first, last):
+        te.matmul(T.pa[:, 0:HALF], stationary(j), buf[:, xap_base:xap_base + HALF], start=first,
+                  stop=last).then_inc(sem.ma, 1)
+        te.matmul(T.pb[:, 0:HALF], stationary(j), buf[:, xap_base + HALF:xap_base + C], start=first,
+                  stop=last).then_inc(sem.mb, 1)
 
     te.wait_ge(sem.wl, 16)
     te.wait_ge(sem.xsl, 16)
     if need_neg:
         te.wait_ge(sem.ng, 1)
-    te.matmul(T.ps[:, :], stationary(r), T.xs[:, :], start=True, stop=False).then_inc(sem.mm, 1)
-    for i, (j, n) in enumerate(arrivals):
-        te.wait_ge(sem["a%d" % j], n)
-        te.matmul(T.ps[:, :], stationary(j), T.land[:, j * C:(j + 1) * C], start=False,
-                  stop=(i == len(arrivals) - 1)).then_inc(sem.mm, 1)
+    product(r, 0, T.xs, True, False)
+    for i, (j, sm, n) in enumerate(arrivals):
+        te.wait_ge(sm, n)
+        product(j, j * C, T.land, False, i == len(arrivals) - 1)
 
-    ve.wait_ge(sem.mm, 1 + len(arrivals))
-    ve.tensor_copy(T.ys[:, :], T.ps[:, :]).then_inc(sem.cp, 1)
-    sy.wait_ge(sem.cp, 1)
+    ve.wait_ge(sem.ma, 1 + len(arrivals))
+    ve.tensor_copy(T.ys[:, 0:HALF], T.pa[:, 0:HALF]).then_inc(sem.cp, 1)
+    ve.wait_ge(sem.mb, 1 + len(arrivals))
+    ve.tensor_copy(T.ys[:, HALF:C], T.pb[:, 0:HALF]).then_inc(sem.cp, 1)
+    sy.wait_ge(sem.cp, 2)
     sy.dma_start(T.y[:, :], T.ys[:, :]).then_inc(sem.st, 16)
     sy.wait_ge(sem.st, 16)
     g.wait_ge(sem.sent, sent)

from concourse.bass import DstId, RemoteDMATransfer
from concourse.mybir import AluOpType

N = 8
C = 128
H = 4
HALF = C // 2
NDRAM = 1

SCRATCH = {
    "hd": ("dram", [128, H], "bfloat16"),
    "bd": ("dram", [128, C - H], "bfloat16"),
    "xd": ("dram", [128, C], "bfloat16"),
    "pl": ("dram", [NDRAM * 128, C], "bfloat16"),
    "xs": ("sbuf", [128, C], "bfloat16"),
    "ws": ("sbuf", [128, C], "bfloat16"),
    "wn": ("sbuf", [128, C], "bfloat16"),
    "m1": ("sbuf", [128, C], "bfloat16"),
    "land": ("sbuf", [128, N * C], "bfloat16"),
    "pa": ("psum", [128, 512], "float32"),
    "pb": ("psum", [128, 512], "float32"),
    "ys": ("sbuf", [128, C], "bfloat16"),
}
SEMAPHORES = (["hl", "bl", "xdl", "xsl", "wl", "ms", "ng", "gh", "gb", "sent", "ma", "mb", "cp", "st"]
              + ["a%d" % j for j in range(N)] + ["sp%d" % i for i in range(NDRAM)])

BODY_ENGINES = 2


def _bits(mask):
    return [e for e in range(mask.bit_length()) if (mask >> e) & 1]


def _mask(engines):
    m = 0
    for e in engines:
        m |= 1 << e
    return m


def _same_chip(topo, a, b):
    return topo.host(a) == topo.host(b) and topo.chip(a) == topo.chip(b)


def _plan(T, topo, s):
    cores = list(T.cores)
    world = range(topo.CORES_PER_HOST * (1 + max(topo.host(c) for c in cores)))
    ring = sorted([s] + [d for d in cores if d != s and topo.may_write(s, d)])
    turn = ring.index(s)
    plane = [ring[(turn + i) % len(ring)] for i in range(1, len(ring))]
    cross = [d for d in cores if d != s and not topo.may_write(s, d)]
    port = [k for k in world if k != s and _same_chip(topo, k, s) and all(topo.may_write(k, d) for d in cross)]
    near = [k for k in port if topo.die(k) == topo.die(s)]
    far = [k for k in port if topo.die(k) != topo.die(s)]
    order = []
    for i in range(max(len(near), len(far))):
        order += near[i:i + 1] + far[i:i + 1]
    via = {}
    for a, d in enumerate(cross):
        via[d] = order[(a + turn) % len(order)]
    return plane, cross, order, via


def rank_program(g, core, T, topo):
    cores = list(T.cores)
    owner = [s for s in cores if _same_chip(topo, s, core)]
    if not owner:
        return
    s = owner[0]
    plane, cross, order, via = _plan(T, topo, s)
    sem = T.sem
    j_own = T.rank_of(s)
    lo = j_own * C
    slot = T.land[:, lo:lo + C]

    if core != s:
        mine = [d for d in cross if via[d] == core]
        if not mine:
            return
        total = 0
        g.wait_ge(sem.gh, 1)
        for d in mine:
            rid, pid = topo.addr(d, core)
            m = topo.mask(core, d)
            g.remote_dma(T.land[:, lo:lo + H], T.hd[:, :], sem["a%d" % j_own], sem.sent, pid, rid, m)
            total += len(_bits(m))
        g.wait_ge(sem.gb, BODY_ENGINES)
        for d in mine:
            rid, pid = topo.addr(d, core)
            m = topo.mask(core, d)
            g.remote_dma(T.land[:, lo + H:lo + C], T.bd[:, :], sem["a%d" % j_own], sem.sent, pid, rid, m)
            total += len(_bits(m))
        g.wait_ge(sem.sent, total)
        return

    r = j_own
    sign = T.tables["SIGN"][r]
    sy, sc, te, ve = g.sync, g.scalar, g.tensor, g.vector

    sy.dma_start(T.hd[:, :], T.x[:, 0:H]).then_inc(sem.hl, 16)
    sy.dma_start(T.xd[:, :], T.x[:, :]).then_inc(sem.xdl, 16)
    sy.dma_start(T.bd[:, :], T.x[:, H:C]).then_inc(sem.bl, 16)
    sc.wait_ge(sem.hl, 16)
    sc.dma_start(T.ws[:, :], T.w[:, :]).then_inc(sem.wl, 16)
    sc.dma_start(T.xs[:, :], T.x[:, :]).then_inc(sem.xsl, 16)

    need_neg = any(v < 0 for v in sign)
    if need_neg:
        ve.memset(T.m1[:, :], -1.0).then_inc(sem.ms, 1)
        ve.wait_ge(sem.ms, 1)
        ve.wait_ge(sem.wl, 16)
        ve.tensor_tensor(T.wn[:, :], T.ws[:, :], T.m1[:, :], AluOpType.mult).then_inc(sem.ng, 1)

    used = [h for h in order if h in via.values()]
    out_mask = topo.mask(s, plane[0])
    for d in plane:
        out_mask &= topo.mask(s, d)
    chip_mask = topo.mask(s, used[0])
    for h in used:
        chip_mask &= topo.mask(s, h)
    eng = _bits(out_mask & chip_mask)
    inner = _bits(chip_mask & ~out_mask)
    sent = 0

    ids = []
    for h in used:
        rid, pid = topo.addr(h, s)
        ids.append(DstId(rid=rid, pnc=pid))
    g.wait_ge(sem.hl, 16)
    g.remote_dma_fused([RemoteDMATransfer(dst_ids=ids, dma_engine_mask=_mask(eng[:1]), remote_sem=sem.gh,
                                          srcs=[T.hd[:, :]], dsts=[T.hd[:, :] for _ in used])], local_sem=sem.sent)
    sent += 1

    ids = []
    dsts = []
    for i, d in enumerate(plane):
        rid, pid = topo.addr(d, s)
        ids.append(DstId(rid=rid, pnc=pid))
        dsts.append(T.pl[i * 128:(i + 1) * 128, :] if i < NDRAM else slot)
    g.wait_ge(sem.xdl, 16)
    g.remote_dma_fused([RemoteDMATransfer(dst_ids=ids, dma_engine_mask=_mask(eng), remote_sem=sem["a%d" % r],
                                          srcs=[T.xd[:, :]], dsts=dsts)], local_sem=sem.sent)
    sent += len(eng)

    g.wait_ge(sem.bl, 16)
    body = []
    group = 2 * BODY_ENGINES
    for q, h in enumerate(used):
        base = (q // 2) * group + (q % 2)
        mine = [inner[(base + 2 * i) % len(inner)] for i in range(BODY_ENGINES)]
        rid, pid = topo.addr(h, s)
        body.append(RemoteDMATransfer(dst_ids=[DstId(rid=rid, pnc=pid)], dma_engine_mask=_mask(mine),
                                      remote_sem=sem.gb, src=T.bd[:, :], dst=T.bd[:, :]))
        sent += len(mine)
    g.remote_dma_fused(body, local_sem=sem.sent)

    before = list(reversed(plane))
    queues = [sy, sc]
    arrivals = []
    spread = []
    for i, d in enumerate(before):
        j = T.rank_of(d)
        if i < NDRAM:
            q = queues[i % len(queues)]
            q.wait_ge(sem["a%d" % j], len(eng))
            q.dma_start(T.land[:, j * C:(j + 1) * C], T.pl[i * 128:(i + 1) * 128, :]).then_inc(sem["sp%d" % i], 16)
            spread.append((j, sem["sp%d" % i], 16))
        else:
            arrivals.append((j, sem["a%d" % j], len(eng)))
    arrivals += spread

    late = []
    for d in cross:
        _, _, order_d, via_d = _plan(T, topo, d)
        h = via_d[s]
        late.append((order_d.index(h), T.rank_of(d), 2 * len(_bits(topo.mask(h, s)))))
    for _, j, n in sorted(late):
        arrivals.append((j, sem["a%d" % j], n))

    def stationary(j):
        return T.ws[:, :] if sign[j] > 0 else T.wn[:, :]

    def product(j, xap_base, buf, first, last):
        te.matmul(T.pa[:, 0:HALF], stationary(j), buf[:, xap_base:xap_base + HALF], start=first,
                  stop=last).then_inc(sem.ma, 1)
        te.matmul(T.pb[:, 0:HALF], stationary(j), buf[:, xap_base + HALF:xap_base + C], start=first,
                  stop=last).then_inc(sem.mb, 1)

    te.wait_ge(sem.wl, 16)
    te.wait_ge(sem.xsl, 16)
    if need_neg:
        te.wait_ge(sem.ng, 1)
    product(r, 0, T.xs, True, False)
    for i, (j, sm, n) in enumerate(arrivals):
        te.wait_ge(sm, n)
        product(j, j * C, T.land, False, i == len(arrivals) - 1)

    ve.wait_ge(sem.ma, 1 + len(arrivals))
    ve.tensor_copy(T.ys[:, 0:HALF], T.pa[:, 0:HALF]).then_inc(sem.cp, 1)
    ve.wait_ge(sem.mb, 1 + len(arrivals))
    ve.tensor_copy(T.ys[:, HALF:C], T.pb[:, 0:HALF]).then_inc(sem.cp, 1)
    sy.wait_ge(sem.cp, 2)
    sy.dma_start(T.y[:, :], T.ys[:, :]).then_inc(sem.st, 16)
    sy.wait_ge(sem.st, 16)
    g.wait_ge(sem.sent, sent)
